import numpy as np
import ml_dtypes


def mxq(x, axis, fmt="e4m3"):
    dtype, down = {"e4m3": (ml_dtypes.float8_e4m3fn, 7), "e5m2": (ml_dtypes.float8_e5m2, 14)}[fmt]
    v = np.moveaxis(np.asarray(x, np.float32).astype(ml_dtypes.bfloat16).astype(np.float64), axis, -1)
    blocks = v.reshape(v.shape[:-1] + (-1, 32))
    amax = np.abs(blocks).max(-1, keepdims=True)
    byte = np.maximum(np.where(amax > 0, np.frexp(amax)[1] - 1 + 127, 0) - down, 1)
    scale = np.exp2(byte - 127.0)
    codes = (blocks / scale).astype(np.float32).astype(dtype).astype(np.float64)
    return np.moveaxis((codes * scale).reshape(v.shape), -1, axis)


WIDE = False


def mx_kscale(k):
    if not WIDE:
        return np.ones(k)
    levels = np.array([10, -10, 5, -5, 0])
    if k % 512:
        return np.exp2(np.random.permutation(np.resize(levels, k // 32))).repeat(32)
    a = np.empty((k // 512, 16))
    for p in range(k // 512):
        a[p, :8] = np.random.permutation(np.resize(levels, 8))
        for g in range(8):
            far = levels[np.abs(levels - a[p, g]) >= 10]
            a[p, g + 8] = far[np.random.randint(len(far))]
    return np.exp2(a.ravel()).repeat(32)


def f64(x):
    return np.asarray(x).astype(np.float64)


def striped(idx):
    return np.tile(idx.reshape(-1, 16).T, (8, 1)).astype(np.uint16)


def unstriped(offs):
    return offs[:16].T.reshape(-1).astype(np.int64)


E2M1 = np.array([0.0, 0.5, 1.0, 1.5, 2.0, 3.0, 4.0, 6.0, -0.0, -0.5, -1.0, -1.5, -2.0, -3.0, -4.0, -6.0])


def pack_weight(w, fmt):
    k, n = w.shape
    w = f64(np.asarray(w, np.float32).astype(ml_dtypes.bfloat16)).reshape(k // 32, 32, n)
    amax = np.abs(w).max(1)
    if fmt == "e4m3":
        byte = np.frexp(amax)[1] - 1 + 127 - 7
    else:
        mant, ex = np.frexp(amax / 6.0)
        byte = np.where(mant > 0.5, ex, ex - 1) + 127
    byte = np.clip(np.where(amax > 0, byte, 1), 1, 254)
    scaled = (w * np.exp2(127.0 - byte)[:, None, :]).reshape(k, n).astype(np.float32)
    by_word = np.ascontiguousarray(scaled.reshape(k // 512, 128, 4, n).transpose(0, 1, 3, 2))
    if fmt == "e4m3":
        words = by_word.astype(ml_dtypes.float8_e4m3fn).view(np.uint8)
    else:
        c = by_word.astype(ml_dtypes.float4_e2m1fn).view(np.uint8) & 0xF
        words = (c[..., 0::2] | (c[..., 1::2] << 4)).reshape(k // 512, 128, 2 * n)
    return np.ascontiguousarray(words), np.ascontiguousarray(byte.astype(np.uint8).reshape(k // 512, 16, n))


def unpack_weight(words, scales, fmt):
    g, _, n = scales.shape
    words = np.ascontiguousarray(words).reshape(g, 128, n, -1)
    if fmt == "e4m3":
        vals = words.view(ml_dtypes.float8_e4m3fn).astype(np.float64)
    else:
        nib = np.empty((g, 128, n, 4), np.uint8)
        nib[..., 0::2] = words & 0xF
        nib[..., 1::2] = words >> 4
        vals = E2M1[nib]
    vals = vals * np.repeat(np.exp2(scales.astype(np.float64) - 127.0), 8, axis=1)[..., None]
    return vals.transpose(0, 1, 3, 2).reshape(g * 512, n)


def pack_table(v):
    words, scales = pack_weight(v, "e4m3")
    return np.concatenate([words.reshape(words.shape[0], -1), scales.reshape(scales.shape[0], -1)], axis=1)


def unpack_table(tab):
    g, t = tab.shape[0], tab.shape[1] // 528
    return unpack_weight(tab[:, :512 * t].reshape(g, 128, t, 4), tab[:, 512 * t:].reshape(g, 16, t), "e4m3")


def silu(v):
    return v / (1.0 + np.exp(-np.maximum(v, -700.0)))


K, M, T, S = 512, 512, 2048, 1024


def setup_inputs():
    n = np.random.standard_normal
    s = mx_kscale(K)[:, None]
    p_w4 = pack_weight(n((K, M)) / np.sqrt(K) / s, "e2m1")
    return {
        "tab": pack_table(n((K, T)) * s),
        "w4_words": p_w4[0],
        "w4_scales": p_w4[1],
        "w8": (n((K, M)) / np.sqrt(K) / s).astype(np.float32),
        "wgo": np.tile(np.random.uniform(0.5, 2.0, S), (128, 1)).astype(np.float32),
        "offs": striped(np.random.permutation(T)[:S]),
        "offs2": striped(np.random.permutation(T)[:S]),
    }


def reference(tab, w4_words, w4_scales, w8, wgo, offs, offs2):
    tab_ = unpack_table(tab)[:, unstriped(offs)]
    w4_ = unpack_weight(w4_words, w4_scales, "e2m1")
    w8_ = mxq(f64(w8), 0, "e4m3")
    y = w4_.T @ tab_
    u = w8_.T @ tab_
    y = silu(y) * u
    out = np.zeros((M, T))
    out[:, unstriped(offs2)] = f64(wgo)[0] * (y)
    return out

@@ -1,0 +1,139 @@
+from contextlib import ExitStack
+
+import concourse.mybir as mybir
+from concourse.masks import make_identity
+
+K, M, T, S = 512, 512, 2048, 1024
+FLOPS = 2 * 2 * K * M * S
+
+F32 = mybir.dt.float32
+BF16 = mybir.dt.bfloat16
+I32 = mybir.dt.int32
+U32 = mybir.dt.uint32
+U16 = mybir.dt.uint16
+U8 = mybir.dt.uint8
+FP8X4 = mybir.dt.float8_e4m3fn_x4
+FP4X4 = mybir.dt.float4_e2m1fn_x4
+ACT = mybir.ActivationFunctionType
+MULT = mybir.AluOpType.mult
+
+P = 128
+PACK = 4
+GATHER = 256
+BANK = 512
+BLOCKS = M // P
+
+
+def tile_list_tabscat_g_none_kernel(tc, tab, w4_words, w4_scales, w8, wgo, offs, offs2, out):
+    nc = tc.nc
+    with ExitStack() as ctx:
+        held = ctx.enter_context(tc.tile_pool(name="held", bufs=1))
+        psum = ctx.enter_context(tc.psum_pool(name="psum", bufs=1))
+
+        pick = held.tile([P, S // 16], U16, name="pick")
+        place = held.tile([P, S // 16], U16, name="place")
+        tab_scales = held.tile([P, T], U8, name="tab_scales", align_bytes=64)
+        gate_scales = held.tile([P, M], U8, name="gate_scales", align_bytes=64)
+        got_words = held.tile([P, S], U32, name="got_words", align_bytes=64)
+        got_scales = held.tile([P, S], U8, name="got_scales", align_bytes=64)
+        ident = held.tile([P, P], F32, name="ident")
+        wgo_cols = held.tile([P, S // P], F32, name="wgo_cols")
+        warm = held.tile([P, 1], F32, name="warm", tag="early", align_bytes=64)
+        pages = [held.tile([P, T], F32, name="page%d" % i) for i in range(2)]
+
+        nc.gpsimd.memset(tab_scales[:].bitcast(I32), 0)
+        make_identity(nc, ident[:])
+        nc.vector.memset(pages[0][:], 0.0)
+        wgo_rows = held.tile([P, P], F32, name="wgo_rows")
+        nc.vector.memset(wgo_rows[:], 0.0)
+        nc.vector.memset(pages[1][:], 0.0)
+        nc.vector.memset(gate_scales[:].bitcast(I32), 0)
+        nc.scalar.activation(warm[:], pages[0][:, 0:1], ACT.Silu)
+
+        w8_rows = w8.rearrange("(p j) n -> p j n", j=PACK)
+        nc.sync.dma_start(pick[:], offs)
+        nc.sync.dma_start(place[:], offs2)
+        scale_rows = tab[0, 512 * T : 528 * T].rearrange("(q t) -> q t", t=T)
+        for q in range(4):
+            nc.scalar.dma_start(tab_scales[32 * q : 32 * q + 4, :].bitcast(I32), scale_rows[4 * q : 4 * q + 4, :].bitcast(I32))
+        raw_first = held.tile([P, PACK, P], F32, name="raw_first", tag="raw")
+        nc.sync.dma_start(raw_first[:], w8_rows[:, :, 0:P])
+        tab_words = held.tile([P, T], I32, name="tab_words", align_bytes=64)
+        nc.sync.dma_start(tab_words[:], tab[0, 0 : 512 * T].rearrange("(p b) -> p b", p=P).bitcast(I32))
+        nc.sync.dma_start(wgo_rows[0 : S // P, :], wgo[0, :].rearrange("(c p) -> c p", p=P))
+        gate_words = held.tile([P, 2 * M], U8, name="gate_words", tag="early", align_bytes=64)
+        nc.sync.dma_start(gate_words[:].bitcast(I32), w4_words[0].bitcast(I32))
+        for q in range(4):
+            nc.sync.dma_start(gate_scales[32 * q : 32 * q + 4, :].bitcast(I32), w4_scales[0, 4 * q : 4 * q + 4, :].bitcast(I32))
+
+        up_words, up_scales = [], []
+
+        def quantise_up(raw, slot):
+            b = len(up_words)
+            woven = held.tile([P, P, PACK], BF16, name="woven%d" % b, tag=slot, align_bytes=64)
+            nc.scalar.copy(woven[:].rearrange("p (c i) j -> p c j i", i=4), raw.rearrange("p j (c i) -> p c j i", i=4))
+            words = held.tile([P, P], U32, name="up_words%d" % b, align_bytes=64)
+            scales = held.tile([P, P], U8, name="up_scales%d" % b, align_bytes=64)
+            nc.vector.quantize_mx(out=words[:].bitcast(FP8X4), scales=scales[:], in_=woven[:].rearrange("p n j -> p (n j)"))
+            up_words.append(words)
+            up_scales.append(scales)
+
+        quantise_up(raw_first[:], "woven")
+        raw_second = held.tile([P, PACK, P], F32, name="raw_second", tag="raw")
+        nc.sync.dma_start(raw_second[:], w8_rows[:, :, P : 2 * P])
+        raw_rest = held.tile([P, PACK, 2 * P], F32, name="raw_rest", tag="woven", align_bytes=64)
+        nc.sync.dma_start(raw_rest[:], w8_rows[:, :, 2 * P : M])
+        raw_next = [raw_second[:], raw_rest[:, :, 0:P], raw_rest[:, :, P : 2 * P]]
+
+        turned = psum.tile([P, 5 * BANK], F32, name="turned", offset=0)
+        nc.tensor.transpose(turned[:, 0:P], wgo_rows[:], ident[:])
+        nc.scalar.copy(wgo_cols[:], turned[:, 0 : S // P])
+
+        for j0 in range(0, S, GATHER):
+            offsets = pick[:, j0 // 16 : (j0 + GATHER) // 16]
+            nc.vector.tensor_copy(got_scales[:, j0 : j0 + GATHER], tab_scales[:].indirect(offsets))
+            nc.vector.tensor_copy(got_words[:, j0 : j0 + GATHER], tab_words[:].bitcast(U32).indirect(offsets))
+
+        units = [(0, j0, GATHER) for j0 in range(0, S, GATHER)] + [(b, j0, BANK) for b in range(1, BLOCKS) for j0 in range(0, S, BANK)]
+        quantise_after = {1: 0, 4: 1, 6: 2}
+        for u, (b, j0, n) in enumerate(units):
+            cols = slice(j0, j0 + n)
+            early = u < 2
+
+            def gate_product():
+                bank = u if early else 3 + u % 2
+                gate = psum.tile([P, n], F32, name="gate%d" % u, offset=4 * BANK * bank)
+                nc.tensor.matmul_mx(out=gate[:], lhsT=gate_words[:, 2 * b * P : 2 * (b + 1) * P].bitcast(FP4X4), lhsT_scale=gate_scales[:, b * P : (b + 1) * P],
+                                    rhs=got_words[:, cols].bitcast(FP8X4), rhs_scale=got_scales[:, cols], start=True, stop=True)
+                return gate
+
+            up_t = psum.tile([P, n // P, P], F32, name="up_t%d" % u, offset=4 * BANK * (u % 3))
+            for c in range(n // P):
+                tok = slice(j0 + c * P, j0 + (c + 1) * P)
+                nc.tensor.matmul_mx(out=up_t[:, c, :], lhsT=got_words[:, tok].bitcast(FP8X4), lhsT_scale=got_scales[:, tok],
+                                    rhs=up_words[b][:].bitcast(FP8X4), rhs_scale=up_scales[b][:], start=True, stop=True)
+            if not early:
+                gate = gate_product()
+            slot = "slot%d" % u if u in quantise_after else "weighted_t%d" % (u % 2)
+            weighted_t = held.tile([P, n // P, P], F32, name="weighted_t%d" % u, tag=slot, align_bytes=64)
+            back = psum.tile([P, n // P, P], F32, name="back%d" % u, offset=4 * BANK * (5 + u % 3))
+            for c in range(n // P):
+                w = j0 // P + c
+                nc.scalar.activation(weighted_t[:, c, :], up_t[:, c, :], ACT.Copy, scale=wgo_cols[:, w : w + 1])
+            for c in range(n // P):
+                nc.tensor.transpose(back[:, c, :], weighted_t[:, c, :], ident[:])
+            gated = held.tile([P, n], F32, name="gated%d" % u)
+            weighted = held.tile([P, n], F32, name="weighted%d" % u, tag="raw" if u == 2 else "weighted%d" % u)
+            if early:
+                gate = gate_product()
+                nc.scalar.copy(weighted[:], back[:].rearrange("p c n -> p (c n)"))
+                nc.scalar.activation(gated[:], gate[:], ACT.Silu)
+            else:
+                nc.scalar.activation(gated[:], gate[:], ACT.Silu)
+                nc.scalar.copy(weighted[:], back[:].rearrange("p c n -> p (c n)"))
+            page = pages[b % 2]
+            nc.vector.tensor_tensor(page[:].indirect(place[:, j0 // 16 : (j0 + n) // 16]), gated[:], weighted[:], MULT)
+            if j0 + n == S:
+                nc.sync.dma_start(out[b * P : (b + 1) * P, :], page[:])
+            if u in quantise_after:
+                quantise_up(raw_next[quantise_after[u]], slot)

@@ -19,8 +19,8 @@ MULT = mybir.AluOpType.mult
 
 P = 128
 PACK = 4
-GATHER = 256
-BANK = 512
+HALF = 512
+BANK_BYTES = 2048
 BLOCKS = M // P
 
 
@@ -28,26 +28,26 @@ def tile_list_tabscat_g_none_kernel(tc, tab, w4_words, w4_scales, w8, wgo, offs,
     nc = tc.nc
     with ExitStack() as ctx:
         held = ctx.enter_context(tc.tile_pool(name="held", bufs=1))
+        shared = ctx.enter_context(tc.tile_pool(name="shared", bufs=1))
         psum = ctx.enter_context(tc.psum_pool(name="psum", bufs=1))
 
         pick = held.tile([P, S // 16], U16, name="pick")
         place = held.tile([P, S // 16], U16, name="place")
+        tab_words = held.tile([P, T], I32, name="tab_words", align_bytes=64)
         tab_scales = held.tile([P, T], U8, name="tab_scales", align_bytes=64)
         gate_scales = held.tile([P, M], U8, name="gate_scales", align_bytes=64)
         got_words = held.tile([P, S], U32, name="got_words", align_bytes=64)
         got_scales = held.tile([P, S], U8, name="got_scales", align_bytes=64)
         ident = held.tile([P, P], F32, name="ident")
         wgo_cols = held.tile([P, S // P], F32, name="wgo_cols")
-        warm = held.tile([P, 1], F32, name="warm", tag="early", align_bytes=64)
+        warm = held.tile([P, 1], F32, name="warm", tag="gate_slot", align_bytes=64)
         pages = [held.tile([P, T], F32, name="page%d" % i) for i in range(2)]
 
         nc.gpsimd.memset(tab_scales[:].bitcast(I32), 0)
         make_identity(nc, ident[:])
         nc.vector.memset(pages[0][:], 0.0)
-        wgo_rows = held.tile([P, P], F32, name="wgo_rows")
-        nc.vector.memset(wgo_rows[:], 0.0)
-        nc.vector.memset(pages[1][:], 0.0)
         nc.vector.memset(gate_scales[:].bitcast(I32), 0)
+        nc.vector.memset(pages[1][:], 0.0)
         nc.scalar.activation(warm[:], pages[0][:, 0:1], ACT.Silu)
 
         w8_rows = w8.rearrange("(p j) n -> p j n", j=PACK)
@@ -56,84 +56,91 @@ def tile_list_tabscat_g_none_kernel(tc, tab, w4_words, w4_scales, w8, wgo, offs,
         scale_rows = tab[0, 512 * T : 528 * T].rearrange("(q t) -> q t", t=T)
         for q in range(4):
             nc.scalar.dma_start(tab_scales[32 * q : 32 * q + 4, :].bitcast(I32), scale_rows[4 * q : 4 * q + 4, :].bitcast(I32))
-        raw_first = held.tile([P, PACK, P], F32, name="raw_first", tag="raw")
+        raw_first = held.tile([P, PACK, P], F32, name="raw_first")
         nc.sync.dma_start(raw_first[:], w8_rows[:, :, 0:P])
-        tab_words = held.tile([P, T], I32, name="tab_words", align_bytes=64)
         nc.sync.dma_start(tab_words[:], tab[0, 0 : 512 * T].rearrange("(p b) -> p b", p=P).bitcast(I32))
-        nc.sync.dma_start(wgo_rows[0 : S // P, :], wgo[0, :].rearrange("(c p) -> c p", p=P))
-        gate_words = held.tile([P, 2 * M], U8, name="gate_words", tag="early", align_bytes=64)
+        gate_words = held.tile([P, 2 * M], U8, name="gate_words", tag="gate_slot", align_bytes=64)
         nc.sync.dma_start(gate_words[:].bitcast(I32), w4_words[0].bitcast(I32))
         for q in range(4):
             nc.sync.dma_start(gate_scales[32 * q : 32 * q + 4, :].bitcast(I32), w4_scales[0, 4 * q : 4 * q + 4, :].bitcast(I32))
 
-        up_words, up_scales = [], []
+        up_words = held.tile([P, M], U32, name="up_words", align_bytes=64)
+        up_scales = held.tile([P, M], U8, name="up_scales", align_bytes=64)
 
-        def quantise_up(raw, slot):
-            b = len(up_words)
-            woven = held.tile([P, P, PACK], BF16, name="woven%d" % b, tag=slot, align_bytes=64)
-            nc.scalar.copy(woven[:].rearrange("p (c i) j -> p c j i", i=4), raw.rearrange("p j (c i) -> p c j i", i=4))
-            words = held.tile([P, P], U32, name="up_words%d" % b, align_bytes=64)
-            scales = held.tile([P, P], U8, name="up_scales%d" % b, align_bytes=64)
-            nc.vector.quantize_mx(out=words[:].bitcast(FP8X4), scales=scales[:], in_=woven[:].rearrange("p n j -> p (n j)"))
-            up_words.append(words)
-            up_scales.append(scales)
+        def quantise_up(raw, woven, n0):
+            width = raw.shape[2]
+            nc.scalar.copy(woven.rearrange("p (c i) j -> p c j i", i=4), raw.rearrange("p j (c i) -> p c j i", i=4))
+            nc.vector.quantize_mx(out=up_words[:, n0 : n0 + width].bitcast(FP8X4), scales=up_scales[:, n0 : n0 + width], in_=woven.rearrange("p n j -> p (n j)"))
 
-        quantise_up(raw_first[:], "woven")
-        raw_second = held.tile([P, PACK, P], F32, name="raw_second", tag="raw")
-        nc.sync.dma_start(raw_second[:], w8_rows[:, :, P : 2 * P])
-        raw_rest = held.tile([P, PACK, 2 * P], F32, name="raw_rest", tag="woven", align_bytes=64)
-        nc.sync.dma_start(raw_rest[:], w8_rows[:, :, 2 * P : M])
-        raw_next = [raw_second[:], raw_rest[:, :, 0:P], raw_rest[:, :, P : 2 * P]]
+        woven_first = shared.tile([P, P, PACK], BF16, name="woven_first", offset=4 * S - 512, align_bytes=64)
+        quantise_up(raw_first[:], woven_first[:], 0)
+        wgo_rows = shared.tile([P, S], F32, name="wgo_rows", offset=0, align_bytes=64)
+        nc.sync.dma_start(wgo_rows[:], wgo)
+        raw_rest = shared.tile([P, PACK, M - P], F32, name="raw_rest", offset=4 * S, align_bytes=64)
+        nc.sync.dma_start(raw_rest[:], w8_rows[:, :, P:M])
 
-        turned = psum.tile([P, 5 * BANK], F32, name="turned", offset=0)
-        nc.tensor.transpose(turned[:, 0:P], wgo_rows[:], ident[:])
-        nc.scalar.copy(wgo_cols[:], turned[:, 0 : S // P])
+        for j0 in range(0, S, HALF):
+            offsets = pick[:, j0 // 16 : (j0 + HALF) // 16]
+            nc.vector.tensor_copy(got_scales[:, j0 : j0 + HALF], tab_scales[:].indirect(offsets))
+            nc.vector.tensor_copy(got_words[:, j0 : j0 + HALF], tab_words[:].bitcast(U32).indirect(offsets))
 
-        for j0 in range(0, S, GATHER):
-            offsets = pick[:, j0 // 16 : (j0 + GATHER) // 16]
-            nc.vector.tensor_copy(got_scales[:, j0 : j0 + GATHER], tab_scales[:].indirect(offsets))
-            nc.vector.tensor_copy(got_words[:, j0 : j0 + GATHER], tab_words[:].bitcast(U32).indirect(offsets))
+        def bank(name, index, shape):
+            return psum.tile(shape, F32, name=name, offset=index * BANK_BYTES)
 
-        units = [(0, j0, GATHER) for j0 in range(0, S, GATHER)] + [(b, j0, BANK) for b in range(1, BLOCKS) for j0 in range(0, S, BANK)]
-        quantise_after = {1: 0, 4: 1, 6: 2}
-        for u, (b, j0, n) in enumerate(units):
-            cols = slice(j0, j0 + n)
-            early = u < 2
+        def gated_half(b, j0, gated_out, index):
+            gate = bank("gate%d_%d" % (b, j0), index, [P, HALF])
+            nc.tensor.matmul_mx(out=gate[:], lhsT=gate_words[:, 2 * b * P : 2 * (b + 1) * P].bitcast(FP4X4), lhsT_scale=gate_scales[:, b * P : (b + 1) * P],
+                                rhs=got_words[:, j0 : j0 + HALF].bitcast(FP8X4), rhs_scale=got_scales[:, j0 : j0 + HALF], start=True, stop=True)
+            nc.scalar.activation(gated_out, gate[:], ACT.Silu)
 
-            def gate_product():
-                bank = u if early else 3 + u % 2
-                gate = psum.tile([P, n], F32, name="gate%d" % u, offset=4 * BANK * bank)
-                nc.tensor.matmul_mx(out=gate[:], lhsT=gate_words[:, 2 * b * P : 2 * (b + 1) * P].bitcast(FP4X4), lhsT_scale=gate_scales[:, b * P : (b + 1) * P],
-                                    rhs=got_words[:, cols].bitcast(FP8X4), rhs_scale=got_scales[:, cols], start=True, stop=True)
-                return gate
-
-            up_t = psum.tile([P, n // P, P], F32, name="up_t%d" % u, offset=4 * BANK * (u % 3))
-            for c in range(n // P):
-                tok = slice(j0 + c * P, j0 + (c + 1) * P)
-                nc.tensor.matmul_mx(out=up_t[:, c, :], lhsT=got_words[:, tok].bitcast(FP8X4), lhsT_scale=got_scales[:, tok],
-                                    rhs=up_words[b][:].bitcast(FP8X4), rhs_scale=up_scales[b][:], start=True, stop=True)
-            if not early:
-                gate = gate_product()
-            slot = "slot%d" % u if u in quantise_after else "weighted_t%d" % (u % 2)
-            weighted_t = held.tile([P, n // P, P], F32, name="weighted_t%d" % u, tag=slot, align_bytes=64)
-            back = psum.tile([P, n // P, P], F32, name="back%d" % u, offset=4 * BANK * (5 + u % 3))
-            for c in range(n // P):
-                w = j0 // P + c
-                nc.scalar.activation(weighted_t[:, c, :], up_t[:, c, :], ACT.Copy, scale=wgo_cols[:, w : w + 1])
-            for c in range(n // P):
-                nc.tensor.transpose(back[:, c, :], weighted_t[:, c, :], ident[:])
-            gated = held.tile([P, n], F32, name="gated%d" % u)
-            weighted = held.tile([P, n], F32, name="weighted%d" % u, tag="raw" if u == 2 else "weighted%d" % u)
-            if early:
-                gate = gate_product()
-                nc.scalar.copy(weighted[:], back[:].rearrange("p c n -> p (c n)"))
-                nc.scalar.activation(gated[:], gate[:], ACT.Silu)
-            else:
-                nc.scalar.activation(gated[:], gate[:], ACT.Silu)
-                nc.scalar.copy(weighted[:], back[:].rearrange("p c n -> p (c n)"))
+        def scatter(b, j0, n, in0, in1):
             page = pages[b % 2]
-            nc.vector.tensor_tensor(page[:].indirect(place[:, j0 // 16 : (j0 + n) // 16]), gated[:], weighted[:], MULT)
+            nc.vector.tensor_tensor(page[:].indirect(place[:, j0 // 16 : (j0 + n) // 16]), in0, in1, MULT)
             if j0 + n == S:
                 nc.sync.dma_start(out[b * P : (b + 1) * P, :], page[:])
-            if u in quantise_after:
-                quantise_up(raw_next[quantise_after[u]], slot)
+
+        for h, j0 in enumerate(range(0, S, HALF)):
+            up = bank("up%d" % h, h, [P, HALF])
+            nc.tensor.matmul_mx(out=up[:], lhsT=up_words[:, 0:P].bitcast(FP8X4), lhsT_scale=up_scales[:, 0:P],
+                                rhs=got_words[:, j0 : j0 + HALF].bitcast(FP8X4), rhs_scale=got_scales[:, j0 : j0 + HALF], start=True, stop=True)
+            gated = held.tile([P, HALF], F32, name="gated0_%d" % h, tag="slot%d" % h, align_bytes=64)
+            gated_half(0, j0, gated[:], 3 + h)
+            product = held.tile([P, HALF], F32, name="product%d" % h, tag="slot0" if h == 1 else "product0", align_bytes=64)
+            nc.vector.tensor_tensor(product[:], up[:], gated[:], MULT)
+            scatter(0, j0, HALF, product[:], wgo_rows[:, j0 : j0 + HALF])
+            if h == 0:
+                woven_rest = held.tile([P, M - P, PACK], BF16, name="woven_rest", tag="slot0", align_bytes=64)
+                quantise_up(raw_rest[:, :, 0:P], woven_rest[:, 0:P, :], P)
+                quantise_up(raw_rest[:, :, P : 3 * P], woven_rest[:, P : 3 * P, :], 2 * P)
+
+        for g in range(2):
+            turned = bank("turned%d" % g, 3 + g, [P, PACK, P])
+            for c in range(PACK):
+                w = PACK * g + c
+                nc.tensor.transpose(turned[:, c, :], wgo_rows[:, w * P : (w + 1) * P], ident[:])
+            nc.scalar.copy(wgo_cols[:, PACK * g : PACK * (g + 1)], turned[:, :, 0])
+
+        u = 0
+        for b in range(1, BLOCKS):
+            width = S if b == BLOCKS - 1 else HALF
+            for s0 in range(0, S, width):
+                gated = held.tile([P, width], F32, name="gated%d_%d" % (b, s0))
+                weighted = held.tile([P, width], F32, name="weighted%d_%d" % (b, s0))
+                for j0 in range(s0, s0 + width, HALF):
+                    cols = slice(j0 - s0, j0 - s0 + HALF)
+                    up_t = bank("up_t%d" % u, (u + 2) % 3, [P, PACK, P])
+                    for c in range(PACK):
+                        tok = slice(j0 + c * P, j0 + (c + 1) * P)
+                        nc.tensor.matmul_mx(out=up_t[:, c, :], lhsT=got_words[:, tok].bitcast(FP8X4), lhsT_scale=got_scales[:, tok],
+                                            rhs=up_words[:, b * P : (b + 1) * P].bitcast(FP8X4), rhs_scale=up_scales[:, b * P : (b + 1) * P], start=True, stop=True)
+                    weighted_t = held.tile([P, PACK, P], F32, name="weighted_t%d" % u, tag="weighted_t%d" % (u % 2))
+                    for c in range(PACK):
+                        w = j0 // P + c
+                        nc.scalar.activation(weighted_t[:, c, :], up_t[:, c, :], ACT.Copy, scale=wgo_cols[:, w : w + 1])
+                    gated_half(b, j0, gated[:, cols], 3 + u % 2)
+                    back = bank("back%d" % u, 5 + (u + 2) % 3, [P, PACK, P])
+                    for c in range(PACK):
+                        nc.tensor.transpose(back[:, c, :], weighted_t[:, c, :], ident[:])
+                    nc.scalar.copy(weighted[:, cols], back[:].rearrange("p c n -> p (c n)"))
+                    u = u + 1
+                scatter(b, s0, width, gated[:], weighted[:])

@@ -20,6 +20,7 @@ MULT = mybir.AluOpType.mult
 P = 128
 PACK = 4
 HALF = 512
+QUARTER = 256
 BANK_BYTES = 2048
 BLOCKS = M // P
 
@@ -40,7 +41,6 @@ def tile_list_tabscat_g_none_kernel(tc, tab, w4_words, w4_scales, w8, wgo, offs,
         got_scales = held.tile([P, S], U8, name="got_scales", align_bytes=64)
         ident = held.tile([P, P], F32, name="ident")
         wgo_cols = held.tile([P, S // P], F32, name="wgo_cols")
-        warm = held.tile([P, 1], F32, name="warm", tag="gate_slot", align_bytes=64)
         pages = [held.tile([P, T], F32, name="page%d" % i) for i in range(2)]
 
         nc.gpsimd.memset(tab_scales[:].bitcast(I32), 0)
@@ -48,7 +48,6 @@ def tile_list_tabscat_g_none_kernel(tc, tab, w4_words, w4_scales, w8, wgo, offs,
         nc.vector.memset(pages[0][:], 0.0)
         nc.vector.memset(gate_scales[:].bitcast(I32), 0)
         nc.vector.memset(pages[1][:], 0.0)
-        nc.scalar.activation(warm[:], pages[0][:, 0:1], ACT.Silu)
 
         w8_rows = w8.rearrange("(p j) n -> p j n", j=PACK)
         nc.sync.dma_start(pick[:], offs)
@@ -56,11 +55,9 @@ def tile_list_tabscat_g_none_kernel(tc, tab, w4_words, w4_scales, w8, wgo, offs,
         scale_rows = tab[0, 512 * T : 528 * T].rearrange("(q t) -> q t", t=T)
         for q in range(4):
             nc.scalar.dma_start(tab_scales[32 * q : 32 * q + 4, :].bitcast(I32), scale_rows[4 * q : 4 * q + 4, :].bitcast(I32))
-        raw_first = held.tile([P, PACK, P], F32, name="raw_first")
+        raw_first = held.tile([P, PACK, P], F32, name="raw_first", tag="gate_slot", align_bytes=64)
         nc.sync.dma_start(raw_first[:], w8_rows[:, :, 0:P])
         nc.sync.dma_start(tab_words[:], tab[0, 0 : 512 * T].rearrange("(p b) -> p b", p=P).bitcast(I32))
-        gate_words = held.tile([P, 2 * M], U8, name="gate_words", tag="gate_slot", align_bytes=64)
-        nc.sync.dma_start(gate_words[:].bitcast(I32), w4_words[0].bitcast(I32))
         for q in range(4):
             nc.sync.dma_start(gate_scales[32 * q : 32 * q + 4, :].bitcast(I32), w4_scales[0, 4 * q : 4 * q + 4, :].bitcast(I32))
 
@@ -74,23 +71,26 @@ def tile_list_tabscat_g_none_kernel(tc, tab, w4_words, w4_scales, w8, wgo, offs,
 
         woven_first = shared.tile([P, P, PACK], BF16, name="woven_first", offset=4 * S - 512, align_bytes=64)
         quantise_up(raw_first[:], woven_first[:], 0)
+        gate_words = held.tile([P, 2 * M], U8, name="gate_words", tag="gate_slot", align_bytes=64)
+        nc.sync.dma_start(gate_words[:].bitcast(I32), w4_words[0].bitcast(I32))
         wgo_rows = shared.tile([P, S], F32, name="wgo_rows", offset=0, align_bytes=64)
         nc.sync.dma_start(wgo_rows[:], wgo)
         raw_rest = shared.tile([P, PACK, M - P], F32, name="raw_rest", offset=4 * S, align_bytes=64)
         nc.sync.dma_start(raw_rest[:], w8_rows[:, :, P:M])
 
+        first_runs = [(0, QUARTER), (QUARTER, QUARTER), (HALF, HALF)]
         for j0 in range(0, S, HALF):
-            offsets = pick[:, j0 // 16 : (j0 + HALF) // 16]
-            nc.vector.tensor_copy(got_scales[:, j0 : j0 + HALF], tab_scales[:].indirect(offsets))
-            nc.vector.tensor_copy(got_words[:, j0 : j0 + HALF], tab_words[:].bitcast(U32).indirect(offsets))
+            nc.vector.tensor_copy(got_scales[:, j0 : j0 + HALF], tab_scales[:].indirect(pick[:, j0 // 16 : (j0 + HALF) // 16]))
+        for j0, n in first_runs:
+            nc.vector.tensor_copy(got_words[:, j0 : j0 + n], tab_words[:].bitcast(U32).indirect(pick[:, j0 // 16 : (j0 + n) // 16]))
 
         def bank(name, index, shape):
             return psum.tile(shape, F32, name=name, offset=index * BANK_BYTES)
 
-        def gated_half(b, j0, gated_out, index):
-            gate = bank("gate%d_%d" % (b, j0), index, [P, HALF])
+        def gated_run(b, j0, n, gated_out, index):
+            gate = bank("gate%d_%d" % (b, j0), index, [P, n])
             nc.tensor.matmul_mx(out=gate[:], lhsT=gate_words[:, 2 * b * P : 2 * (b + 1) * P].bitcast(FP4X4), lhsT_scale=gate_scales[:, b * P : (b + 1) * P],
-                                rhs=got_words[:, j0 : j0 + HALF].bitcast(FP8X4), rhs_scale=got_scales[:, j0 : j0 + HALF], start=True, stop=True)
+                                rhs=got_words[:, j0 : j0 + n].bitcast(FP8X4), rhs_scale=got_scales[:, j0 : j0 + n], start=True, stop=True)
             nc.scalar.activation(gated_out, gate[:], ACT.Silu)
 
         def scatter(b, j0, n, in0, in1):
@@ -99,26 +99,32 @@ def tile_list_tabscat_g_none_kernel(tc, tab, w4_words, w4_scales, w8, wgo, offs,
             if j0 + n == S:
                 nc.sync.dma_start(out[b * P : (b + 1) * P, :], page[:])
 
-        for h, j0 in enumerate(range(0, S, HALF)):
-            up = bank("up%d" % h, h, [P, HALF])
+        def first_block_run(j0, n, gated, product_out, gate_bank, up_bank):
+            gated_run(0, j0, n, gated[:], gate_bank)
+            up = bank("up%d" % j0, up_bank, [P, n])
             nc.tensor.matmul_mx(out=up[:], lhsT=up_words[:, 0:P].bitcast(FP8X4), lhsT_scale=up_scales[:, 0:P],
-                                rhs=got_words[:, j0 : j0 + HALF].bitcast(FP8X4), rhs_scale=got_scales[:, j0 : j0 + HALF], start=True, stop=True)
-            gated = held.tile([P, HALF], F32, name="gated0_%d" % h, tag="slot%d" % h, align_bytes=64)
-            gated_half(0, j0, gated[:], 3 + h)
-            product = held.tile([P, HALF], F32, name="product%d" % h, tag="slot0" if h == 1 else "product0", align_bytes=64)
-            nc.vector.tensor_tensor(product[:], up[:], gated[:], MULT)
-            scatter(0, j0, HALF, product[:], wgo_rows[:, j0 : j0 + HALF])
-            if h == 0:
-                woven_rest = held.tile([P, M - P, PACK], BF16, name="woven_rest", tag="slot0", align_bytes=64)
-                quantise_up(raw_rest[:, :, 0:P], woven_rest[:, 0:P, :], P)
-                quantise_up(raw_rest[:, :, P : 3 * P], woven_rest[:, P : 3 * P, :], 2 * P)
+                                rhs=got_words[:, j0 : j0 + n].bitcast(FP8X4), rhs_scale=got_scales[:, j0 : j0 + n], start=True, stop=True)
+            nc.vector.tensor_tensor(product_out, up[:], gated[:], MULT)
 
-        for g in range(2):
-            turned = bank("turned%d" % g, 3 + g, [P, PACK, P])
-            for c in range(PACK):
-                w = PACK * g + c
-                nc.tensor.transpose(turned[:, c, :], wgo_rows[:, w * P : (w + 1) * P], ident[:])
-            nc.scalar.copy(wgo_cols[:, PACK * g : PACK * (g + 1)], turned[:, :, 0])
+        product = held.tile([P, HALF], F32, name="product0")
+        gated = held.tile([P, QUARTER], F32, name="gated0_0")
+        first_block_run(0, QUARTER, gated, product[:, 0:QUARTER], 3, 0)
+        gated = held.tile([P, QUARTER], F32, name="gated0_1", tag="woven_slot", align_bytes=64)
+        first_block_run(QUARTER, QUARTER, gated, product[:, QUARTER:HALF], 4, 3)
+        scatter(0, 0, HALF, product[:], wgo_rows[:, 0:HALF])
+        woven_rest = held.tile([P, M - P, PACK], BF16, name="woven_rest", tag="woven_slot", align_bytes=64)
+        quantise_up(raw_rest[:, :, 0:P], woven_rest[:, 0:P, :], P)
+        quantise_up(raw_rest[:, :, P : 3 * P], woven_rest[:, P : 3 * P, :], 2 * P)
+        product = held.tile([P, HALF], F32, name="product1", tag="woven_slot", align_bytes=64)
+        gated = held.tile([P, HALF], F32, name="gated0_2")
+        first_block_run(HALF, HALF, gated, product[:], 0, 4)
+        scatter(0, HALF, HALF, product[:], wgo_rows[:, HALF:S])
+
+        turned = bank("turned", 2, [P, S // P, P])
+        for w in range(S // P):
+            nc.tensor.transpose(turned[:, w, :], wgo_rows[:, w * P : (w + 1) * P], ident[:])
+        for w in range(0, S // P, PACK):
+            nc.scalar.copy(wgo_cols[:, w : w + PACK], turned[:, w : w + PACK, 0])
 
         u = 0
         for b in range(1, BLOCKS):
@@ -137,7 +143,7 @@ def tile_list_tabscat_g_none_kernel(tc, tab, w4_words, w4_scales, w8, wgo, offs,
                     for c in range(PACK):
                         w = j0 // P + c
                         nc.scalar.activation(weighted_t[:, c, :], up_t[:, c, :], ACT.Copy, scale=wgo_cols[:, w : w + 1])
-                    gated_half(b, j0, gated[:, cols], 3 + u % 2)
+                    gated_run(b, j0, HALF, gated[:, cols], 3 + u % 2)
                     back = bank("back%d" % u, 5 + (u + 2) % 3, [P, PACK, P])
                     for c in range(PACK):
                         nc.tensor.transpose(back[:, c, :], weighted_t[:, c, :], ident[:])

@@ -30,34 +30,39 @@ def tile_list_tabscat_g_none_kernel(tc, tab, w4_words, w4_scales, w8, wgo, offs,
     with ExitStack() as ctx:
         held = ctx.enter_context(tc.tile_pool(name="held", bufs=1))
         shared = ctx.enter_context(tc.tile_pool(name="shared", bufs=1))
+        early = ctx.enter_context(tc.tile_pool(name="early", bufs=1))
         psum = ctx.enter_context(tc.psum_pool(name="psum", bufs=1))
 
         pick = held.tile([P, S // 16], U16, name="pick")
         place = held.tile([P, S // 16], U16, name="place")
-        tab_words = held.tile([P, T], I32, name="tab_words", align_bytes=64)
         tab_scales = held.tile([P, T], U8, name="tab_scales", align_bytes=64)
-        gate_scales = held.tile([P, M], U8, name="gate_scales", align_bytes=64)
         got_words = held.tile([P, S], U32, name="got_words", align_bytes=64)
         got_scales = held.tile([P, S], U8, name="got_scales", align_bytes=64)
         ident = held.tile([P, P], F32, name="ident")
         wgo_cols = held.tile([P, S // P], F32, name="wgo_cols")
         pages = [held.tile([P, T], F32, name="page%d" % i) for i in range(2)]
 
-        nc.gpsimd.memset(tab_scales[:].bitcast(I32), 0)
+        nc.vector.memset(tab_scales[:].bitcast(I32), 0)
         make_identity(nc, ident[:])
         nc.vector.memset(pages[0][:], 0.0)
-        nc.vector.memset(gate_scales[:].bitcast(I32), 0)
+        warm = early.tile([P, (2 * M + 128) // 4], F32, name="warm", offset=M - 64, align_bytes=64)
+        nc.scalar.activation(warm[:, 0:1], pages[0][:, 0:1], ACT.Silu)
         nc.vector.memset(pages[1][:], 0.0)
+        gate_scales = early.tile([P, M], U8, name="gate_scales", offset=0, align_bytes=64)
+        gate_words = early.tile([P, 2 * M], U8, name="gate_words", offset=M, align_bytes=64)
+        tab_words = early.tile([P, T], I32, name="tab_words", offset=3 * M, align_bytes=64)
+        nc.vector.memset(gate_scales[:].bitcast(I32), 0)
 
         w8_rows = w8.rearrange("(p j) n -> p j n", j=PACK)
         nc.sync.dma_start(pick[:], offs)
         nc.sync.dma_start(place[:], offs2)
         scale_rows = tab[0, 512 * T : 528 * T].rearrange("(q t) -> q t", t=T)
         for q in range(4):
-            nc.scalar.dma_start(tab_scales[32 * q : 32 * q + 4, :].bitcast(I32), scale_rows[4 * q : 4 * q + 4, :].bitcast(I32))
-        raw_first = held.tile([P, PACK, P], F32, name="raw_first", tag="gate_slot", align_bytes=64)
+            nc.sync.dma_start(tab_scales[32 * q : 32 * q + 4, :].bitcast(I32), scale_rows[4 * q : 4 * q + 4, :].bitcast(I32))
+        raw_first = held.tile([P, PACK, P], F32, name="raw_first")
         nc.sync.dma_start(raw_first[:], w8_rows[:, :, 0:P])
         nc.sync.dma_start(tab_words[:], tab[0, 0 : 512 * T].rearrange("(p b) -> p b", p=P).bitcast(I32))
+        nc.sync.dma_start(gate_words[:].bitcast(I32), w4_words[0].bitcast(I32))
         for q in range(4):
             nc.sync.dma_start(gate_scales[32 * q : 32 * q + 4, :].bitcast(I32), w4_scales[0, 4 * q : 4 * q + 4, :].bitcast(I32))
 
@@ -71,8 +76,6 @@ def tile_list_tabscat_g_none_kernel(tc, tab, w4_words, w4_scales, w8, wgo, offs,
 
         woven_first = shared.tile([P, P, PACK], BF16, name="woven_first", offset=4 * S - 512, align_bytes=64)
         quantise_up(raw_first[:], woven_first[:], 0)
-        gate_words = held.tile([P, 2 * M], U8, name="gate_words", tag="gate_slot", align_bytes=64)
-        nc.sync.dma_start(gate_words[:].bitcast(I32), w4_words[0].bitcast(I32))
         wgo_rows = shared.tile([P, S], F32, name="wgo_rows", offset=0, align_bytes=64)
         nc.sync.dma_start(wgo_rows[:], wgo)
         raw_rest = shared.tile([P, PACK, M - P], F32, name="raw_rest", offset=4 * S, align_bytes=64)

@@ -19,8 +19,11 @@ MULT = mybir.AluOpType.mult
 
 P = 128
 PACK = 4
+QUADRANTS = 4
+PER_COLUMN = 16
 HALF = 512
 QUARTER = 256
+LINE = 4
 BANK_BYTES = 2048
 BLOCKS = M // P
 
@@ -31,48 +34,48 @@ def tile_list_tabscat_g_none_kernel(tc, tab, w4_words, w4_scales, w8, wgo, offs,
         held = ctx.enter_context(tc.tile_pool(name="held", bufs=1))
         shared = ctx.enter_context(tc.tile_pool(name="shared", bufs=1))
         early = ctx.enter_context(tc.tile_pool(name="early", bufs=1))
+        late = ctx.enter_context(tc.tile_pool(name="late", bufs=1))
         psum = ctx.enter_context(tc.psum_pool(name="psum", bufs=1))
 
-        pick = held.tile([P, S // 16], U16, name="pick")
-        place = held.tile([P, S // 16], U16, name="place")
+        pick = held.tile([P, S // PER_COLUMN], U16, name="pick")
+        place = held.tile([P, S // PER_COLUMN], U16, name="place")
         tab_scales = held.tile([P, T], U8, name="tab_scales", align_bytes=64)
         got_words = held.tile([P, S], U32, name="got_words", align_bytes=64)
         got_scales = held.tile([P, S], U8, name="got_scales", align_bytes=64)
         ident = held.tile([P, P], F32, name="ident")
         wgo_cols = held.tile([P, S // P], F32, name="wgo_cols")
-        pages = [held.tile([P, T], F32, name="page%d" % i) for i in range(2)]
+        gate_scales = held.tile([P, M], U8, name="gate_scales", align_bytes=64)
+        pages = [held.tile([P, T], F32, name="page0"), late.tile([P, T], F32, name="page1", offset=0)]
 
         nc.vector.memset(tab_scales[:].bitcast(I32), 0)
         make_identity(nc, ident[:])
+        filler = early.tile([P, M // 4], I32, name="filler", offset=2 * M - M // 2, align_bytes=64)
+        nc.vector.memset(filler[:], 0)
+        nc.vector.tensor_copy(gate_scales[:].bitcast(I32), filler[:])
         nc.vector.memset(pages[0][:], 0.0)
-        warm = early.tile([P, (2 * M + 128) // 4], F32, name="warm", offset=M - 64, align_bytes=64)
-        nc.scalar.activation(warm[:, 0:1], pages[0][:, 0:1], ACT.Silu)
-        nc.vector.memset(pages[1][:], 0.0)
-        gate_scales = early.tile([P, M], U8, name="gate_scales", offset=0, align_bytes=64)
-        gate_words = early.tile([P, 2 * M], U8, name="gate_words", offset=M, align_bytes=64)
-        tab_words = early.tile([P, T], I32, name="tab_words", offset=3 * M, align_bytes=64)
-        nc.vector.memset(gate_scales[:].bitcast(I32), 0)
+        gate_words = early.tile([P, 2 * M], U8, name="gate_words", offset=0, align_bytes=64)
+        tab_words = early.tile([P, T], I32, name="tab_words", offset=2 * M, align_bytes=64)
 
-        w8_rows = w8.rearrange("(p j) n -> p j n", j=PACK)
+        w8_rows = w8.rearrange("(p i) n -> p i n", i=PACK)
         nc.sync.dma_start(pick[:], offs)
         nc.sync.dma_start(place[:], offs2)
-        scale_rows = tab[0, 512 * T : 528 * T].rearrange("(q t) -> q t", t=T)
-        for q in range(4):
-            nc.sync.dma_start(tab_scales[32 * q : 32 * q + 4, :].bitcast(I32), scale_rows[4 * q : 4 * q + 4, :].bitcast(I32))
+        scale_rows = tab[0, K * T : (K + K // 32) * T].rearrange("(q t) -> q t", t=T)
+        for quad in range(QUADRANTS):
+            nc.sync.dma_start(tab_scales[32 * quad : 32 * quad + 4, :].bitcast(I32), scale_rows[4 * quad : 4 * quad + 4, :].bitcast(I32))
         raw_first = held.tile([P, PACK, P], F32, name="raw_first")
         nc.sync.dma_start(raw_first[:], w8_rows[:, :, 0:P])
-        nc.sync.dma_start(tab_words[:], tab[0, 0 : 512 * T].rearrange("(p b) -> p b", p=P).bitcast(I32))
+        nc.sync.dma_start(tab_words[:], tab[0, 0 : K * T].rearrange("(p b) -> p b", p=P).bitcast(I32))
         nc.sync.dma_start(gate_words[:].bitcast(I32), w4_words[0].bitcast(I32))
-        for q in range(4):
-            nc.sync.dma_start(gate_scales[32 * q : 32 * q + 4, :].bitcast(I32), w4_scales[0, 4 * q : 4 * q + 4, :].bitcast(I32))
+        for quad in range(QUADRANTS):
+            nc.sync.dma_start(gate_scales[32 * quad : 32 * quad + 4, :].bitcast(I32), w4_scales[0, 4 * quad : 4 * quad + 4, :].bitcast(I32))
 
         up_words = held.tile([P, M], U32, name="up_words", align_bytes=64)
         up_scales = held.tile([P, M], U8, name="up_scales", align_bytes=64)
 
         def quantise_up(raw, woven, n0):
             width = raw.shape[2]
-            nc.scalar.copy(woven.rearrange("p (c i) j -> p c j i", i=4), raw.rearrange("p j (c i) -> p c j i", i=4))
-            nc.vector.quantize_mx(out=up_words[:, n0 : n0 + width].bitcast(FP8X4), scales=up_scales[:, n0 : n0 + width], in_=woven.rearrange("p n j -> p (n j)"))
+            nc.scalar.copy(woven.rearrange("p (c e) i -> p c i e", e=LINE), raw.rearrange("p i (c e) -> p c i e", e=LINE))
+            nc.vector.quantize_mx(out=up_words[:, n0 : n0 + width].bitcast(FP8X4), scales=up_scales[:, n0 : n0 + width], in_=woven.rearrange("p n i -> p (n i)"))
 
         woven_first = shared.tile([P, P, PACK], BF16, name="woven_first", offset=4 * S - 512, align_bytes=64)
         quantise_up(raw_first[:], woven_first[:], 0)
@@ -81,24 +84,26 @@ def tile_list_tabscat_g_none_kernel(tc, tab, w4_words, w4_scales, w8, wgo, offs,
         raw_rest = shared.tile([P, PACK, M - P], F32, name="raw_rest", offset=4 * S, align_bytes=64)
         nc.sync.dma_start(raw_rest[:], w8_rows[:, :, P:M])
 
-        first_runs = [(0, QUARTER), (QUARTER, QUARTER), (HALF, HALF)]
+        def entries(list_tile, j0, n):
+            return list_tile[:, j0 // PER_COLUMN : (j0 + n) // PER_COLUMN]
+
         for j0 in range(0, S, HALF):
-            nc.vector.tensor_copy(got_scales[:, j0 : j0 + HALF], tab_scales[:].indirect(pick[:, j0 // 16 : (j0 + HALF) // 16]))
-        for j0, n in first_runs:
-            nc.vector.tensor_copy(got_words[:, j0 : j0 + n], tab_words[:].bitcast(U32).indirect(pick[:, j0 // 16 : (j0 + n) // 16]))
+            nc.vector.tensor_copy(got_scales[:, j0 : j0 + HALF], tab_scales[:].indirect(entries(pick, j0, HALF)))
+        for j0, n in [(0, QUARTER), (QUARTER, QUARTER), (HALF, HALF)]:
+            nc.vector.tensor_copy(got_words[:, j0 : j0 + n], tab_words[:].bitcast(U32).indirect(entries(pick, j0, n)))
 
         def bank(name, index, shape):
             return psum.tile(shape, F32, name=name, offset=index * BANK_BYTES)
 
-        def gated_run(b, j0, n, gated_out, index):
-            gate = bank("gate%d_%d" % (b, j0), index, [P, n])
+        def gated_run(b, j0, n, gated_out, gate_bank):
+            gate = bank("gate%d_%d" % (b, j0), gate_bank, [P, n])
             nc.tensor.matmul_mx(out=gate[:], lhsT=gate_words[:, 2 * b * P : 2 * (b + 1) * P].bitcast(FP4X4), lhsT_scale=gate_scales[:, b * P : (b + 1) * P],
                                 rhs=got_words[:, j0 : j0 + n].bitcast(FP8X4), rhs_scale=got_scales[:, j0 : j0 + n], start=True, stop=True)
             nc.scalar.activation(gated_out, gate[:], ACT.Silu)
 
         def scatter(b, j0, n, in0, in1):
             page = pages[b % 2]
-            nc.vector.tensor_tensor(page[:].indirect(place[:, j0 // 16 : (j0 + n) // 16]), in0, in1, MULT)
+            nc.vector.tensor_tensor(page[:].indirect(entries(place, j0, n)), in0, in1, MULT)
             if j0 + n == S:
                 nc.sync.dma_start(out[b * P : (b + 1) * P, :], page[:])
 
@@ -110,46 +115,47 @@ def tile_list_tabscat_g_none_kernel(tc, tab, w4_words, w4_scales, w8, wgo, offs,
             nc.vector.tensor_tensor(product_out, up[:], gated[:], MULT)
 
         product = held.tile([P, HALF], F32, name="product0")
-        gated = held.tile([P, QUARTER], F32, name="gated0_0")
-        first_block_run(0, QUARTER, gated, product[:, 0:QUARTER], 3, 0)
+        gated = late.tile([P, QUARTER], F32, name="gated0_0", offset=0)
+        first_block_run(0, QUARTER, gated, product[:, 0:QUARTER], gate_bank=3, up_bank=0)
+        nc.gpsimd.memset(pages[1][:], 0.0)
         gated = held.tile([P, QUARTER], F32, name="gated0_1", tag="woven_slot", align_bytes=64)
-        first_block_run(QUARTER, QUARTER, gated, product[:, QUARTER:HALF], 4, 3)
+        first_block_run(QUARTER, QUARTER, gated, product[:, QUARTER:HALF], gate_bank=4, up_bank=3)
         scatter(0, 0, HALF, product[:], wgo_rows[:, 0:HALF])
         woven_rest = held.tile([P, M - P, PACK], BF16, name="woven_rest", tag="woven_slot", align_bytes=64)
         quantise_up(raw_rest[:, :, 0:P], woven_rest[:, 0:P, :], P)
         quantise_up(raw_rest[:, :, P : 3 * P], woven_rest[:, P : 3 * P, :], 2 * P)
         product = held.tile([P, HALF], F32, name="product1", tag="woven_slot", align_bytes=64)
         gated = held.tile([P, HALF], F32, name="gated0_2")
-        first_block_run(HALF, HALF, gated, product[:], 0, 4)
+        first_block_run(HALF, HALF, gated, product[:], gate_bank=0, up_bank=4)
         scatter(0, HALF, HALF, product[:], wgo_rows[:, HALF:S])
 
         turned = bank("turned", 2, [P, S // P, P])
         for w in range(S // P):
             nc.tensor.transpose(turned[:, w, :], wgo_rows[:, w * P : (w + 1) * P], ident[:])
-        for w in range(0, S // P, PACK):
-            nc.scalar.copy(wgo_cols[:, w : w + PACK], turned[:, w : w + PACK, 0])
+        for w in range(0, S // P, HALF // P):
+            nc.scalar.copy(wgo_cols[:, w : w + HALF // P], turned[:, w : w + HALF // P, 0])
 
-        u = 0
+        step = 0
         for b in range(1, BLOCKS):
-            width = S if b == BLOCKS - 1 else HALF
+            width = HALF if b == 1 else S
             for s0 in range(0, S, width):
                 gated = held.tile([P, width], F32, name="gated%d_%d" % (b, s0))
                 weighted = held.tile([P, width], F32, name="weighted%d_%d" % (b, s0))
                 for j0 in range(s0, s0 + width, HALF):
                     cols = slice(j0 - s0, j0 - s0 + HALF)
-                    up_t = bank("up_t%d" % u, (u + 2) % 3, [P, PACK, P])
-                    for c in range(PACK):
-                        tok = slice(j0 + c * P, j0 + (c + 1) * P)
-                        nc.tensor.matmul_mx(out=up_t[:, c, :], lhsT=got_words[:, tok].bitcast(FP8X4), lhsT_scale=got_scales[:, tok],
+                    up_t = bank("up_t%d" % step, (step + 2) % 3, [P, HALF // P, P])
+                    for c in range(HALF // P):
+                        picked = slice(j0 + c * P, j0 + (c + 1) * P)
+                        nc.tensor.matmul_mx(out=up_t[:, c, :], lhsT=got_words[:, picked].bitcast(FP8X4), lhsT_scale=got_scales[:, picked],
                                             rhs=up_words[:, b * P : (b + 1) * P].bitcast(FP8X4), rhs_scale=up_scales[:, b * P : (b + 1) * P], start=True, stop=True)
-                    weighted_t = held.tile([P, PACK, P], F32, name="weighted_t%d" % u, tag="weighted_t%d" % (u % 2))
-                    for c in range(PACK):
+                    weighted_t = held.tile([P, HALF // P, P], F32, name="weighted_t%d" % step, tag="weighted_t%d" % (step % 2))
+                    for c in range(HALF // P):
                         w = j0 // P + c
                         nc.scalar.activation(weighted_t[:, c, :], up_t[:, c, :], ACT.Copy, scale=wgo_cols[:, w : w + 1])
-                    gated_run(b, j0, HALF, gated[:, cols], 3 + u % 2)
-                    back = bank("back%d" % u, 5 + (u + 2) % 3, [P, PACK, P])
-                    for c in range(PACK):
+                    gated_run(b, j0, HALF, gated[:, cols], 3 + step % 2)
+                    back = bank("back%d" % step, 5 + (step + 2) % 3, [P, HALF // P, P])
+                    for c in range(HALF // P):
                         nc.tensor.transpose(back[:, c, :], weighted_t[:, c, :], ident[:])
                     nc.scalar.copy(weighted[:, cols], back[:].rearrange("p c n -> p (c n)"))
-                    u = u + 1
+                    step = step + 1
                 scatter(b, s0, width, gated[:], weighted[:])

from contextlib import ExitStack

import concourse.mybir as mybir
from concourse.masks import make_identity

K, M, T, S = 512, 512, 2048, 1024
FLOPS = 2 * 2 * K * M * S

F32 = mybir.dt.float32
BF16 = mybir.dt.bfloat16
I32 = mybir.dt.int32
U32 = mybir.dt.uint32
U16 = mybir.dt.uint16
U8 = mybir.dt.uint8
FP8X4 = mybir.dt.float8_e4m3fn_x4
FP4X4 = mybir.dt.float4_e2m1fn_x4
ACT = mybir.ActivationFunctionType
MULT = mybir.AluOpType.mult

P = 128
PACK = 4
QUADRANTS = 4
PER_COLUMN = 16
HALF = 512
QUARTER = 256
LINE = 4
BANK_BYTES = 2048
BLOCKS = M // P


def tile_list_tabscat_g_none_kernel(tc, tab, w4_words, w4_scales, w8, wgo, offs, offs2, out):
    nc = tc.nc
    with ExitStack() as ctx:
        held = ctx.enter_context(tc.tile_pool(name="held", bufs=1))
        shared = ctx.enter_context(tc.tile_pool(name="shared", bufs=1))
        early = ctx.enter_context(tc.tile_pool(name="early", bufs=1))
        late = ctx.enter_context(tc.tile_pool(name="late", bufs=1))
        psum = ctx.enter_context(tc.psum_pool(name="psum", bufs=1))

        pick = held.tile([P, S // PER_COLUMN], U16, name="pick")
        place = held.tile([P, S // PER_COLUMN], U16, name="place")
        tab_scales = held.tile([P, T], U8, name="tab_scales", align_bytes=64)
        got_words = held.tile([P, S], U32, name="got_words", align_bytes=64)
        got_scales = held.tile([P, S], U8, name="got_scales", align_bytes=64)
        ident = held.tile([P, P], F32, name="ident")
        wgo_cols = held.tile([P, S // P], F32, name="wgo_cols")
        gate_scales = held.tile([P, M], U8, name="gate_scales", align_bytes=64)
        pages = [held.tile([P, T], F32, name="page0"), late.tile([P, T], F32, name="page1", offset=0)]

        nc.vector.memset(tab_scales[:].bitcast(I32), 0)
        make_identity(nc, ident[:])
        filler = early.tile([P, M // 4], I32, name="filler", offset=2 * M - M // 2, align_bytes=64)
        nc.vector.memset(filler[:], 0)
        nc.vector.tensor_copy(gate_scales[:].bitcast(I32), filler[:])
        nc.vector.memset(pages[0][:], 0.0)
        gate_words = early.tile([P, 2 * M], U8, name="gate_words", offset=0, align_bytes=64)
        tab_words = early.tile([P, T], I32, name="tab_words", offset=2 * M, align_bytes=64)

        w8_rows = w8.rearrange("(p i) n -> p i n", i=PACK)
        nc.sync.dma_start(pick[:], offs)
        nc.sync.dma_start(place[:], offs2)
        scale_rows = tab[0, K * T : (K + K // 32) * T].rearrange("(q t) -> q t", t=T)
        for quad in range(QUADRANTS):
            nc.sync.dma_start(tab_scales[32 * quad : 32 * quad + 4, :].bitcast(I32), scale_rows[4 * quad : 4 * quad + 4, :].bitcast(I32))
        raw_first = held.tile([P, PACK, P], F32, name="raw_first")
        nc.sync.dma_start(raw_first[:], w8_rows[:, :, 0:P])
        nc.sync.dma_start(tab_words[:], tab[0, 0 : K * T].rearrange("(p b) -> p b", p=P).bitcast(I32))
        nc.sync.dma_start(gate_words[:].bitcast(I32), w4_words[0].bitcast(I32))
        for quad in range(QUADRANTS):
            nc.sync.dma_start(gate_scales[32 * quad : 32 * quad + 4, :].bitcast(I32), w4_scales[0, 4 * quad : 4 * quad + 4, :].bitcast(I32))

        up_words = held.tile([P, M], U32, name="up_words", align_bytes=64)
        up_scales = held.tile([P, M], U8, name="up_scales", align_bytes=64)

        def quantise_up(raw, woven, n0):
            width = raw.shape[2]
            nc.scalar.copy(woven.rearrange("p (c e) i -> p c i e", e=LINE), raw.rearrange("p i (c e) -> p c i e", e=LINE))
            nc.vector.quantize_mx(out=up_words[:, n0 : n0 + width].bitcast(FP8X4), scales=up_scales[:, n0 : n0 + width], in_=woven.rearrange("p n i -> p (n i)"))

        woven_first = shared.tile([P, P, PACK], BF16, name="woven_first", offset=4 * S - 512, align_bytes=64)
        quantise_up(raw_first[:], woven_first[:], 0)
        wgo_rows = shared.tile([P, S], F32, name="wgo_rows", offset=0, align_bytes=64)
        nc.sync.dma_start(wgo_rows[:], wgo)
        raw_rest = shared.tile([P, PACK, M - P], F32, name="raw_rest", offset=4 * S, align_bytes=64)
        nc.sync.dma_start(raw_rest[:], w8_rows[:, :, P:M])

        def entries(list_tile, j0, n):
            return list_tile[:, j0 // PER_COLUMN : (j0 + n) // PER_COLUMN]

        for j0 in range(0, S, HALF):
            nc.vector.tensor_copy(got_scales[:, j0 : j0 + HALF], tab_scales[:].indirect(entries(pick, j0, HALF)))
        for j0, n in [(0, QUARTER), (QUARTER, QUARTER), (HALF, HALF)]:
            nc.vector.tensor_copy(got_words[:, j0 : j0 + n], tab_words[:].bitcast(U32).indirect(entries(pick, j0, n)))

        def bank(name, index, shape):
            return psum.tile(shape, F32, name=name, offset=index * BANK_BYTES)

        def gated_run(b, j0, n, gated_out, gate_bank):
            gate = bank("gate%d_%d" % (b, j0), gate_bank, [P, n])
            nc.tensor.matmul_mx(out=gate[:], lhsT=gate_words[:, 2 * b * P : 2 * (b + 1) * P].bitcast(FP4X4), lhsT_scale=gate_scales[:, b * P : (b + 1) * P],
                                rhs=got_words[:, j0 : j0 + n].bitcast(FP8X4), rhs_scale=got_scales[:, j0 : j0 + n], start=True, stop=True)
            nc.scalar.activation(gated_out, gate[:], ACT.Silu)

        def scatter(b, j0, n, in0, in1):
            page = pages[b % 2]
            nc.vector.tensor_tensor(page[:].indirect(entries(place, j0, n)), in0, in1, MULT)
            if j0 + n == S:
                nc.sync.dma_start(out[b * P : (b + 1) * P, :], page[:])

        def first_block_run(j0, n, gated, product_out, gate_bank, up_bank):
            gated_run(0, j0, n, gated[:], gate_bank)
            up = bank("up%d" % j0, up_bank, [P, n])
            nc.tensor.matmul_mx(out=up[:], lhsT=up_words[:, 0:P].bitcast(FP8X4), lhsT_scale=up_scales[:, 0:P],
                                rhs=got_words[:, j0 : j0 + n].bitcast(FP8X4), rhs_scale=got_scales[:, j0 : j0 + n], start=True, stop=True)
            nc.vector.tensor_tensor(product_out, up[:], gated[:], MULT)

        product = held.tile([P, HALF], F32, name="product0")
        gated = late.tile([P, QUARTER], F32, name="gated0_0", offset=0)
        first_block_run(0, QUARTER, gated, product[:, 0:QUARTER], gate_bank=3, up_bank=0)
        nc.gpsimd.memset(pages[1][:], 0.0)
        gated = held.tile([P, QUARTER], F32, name="gated0_1", tag="woven_slot", align_bytes=64)
        first_block_run(QUARTER, QUARTER, gated, product[:, QUARTER:HALF], gate_bank=4, up_bank=3)
        scatter(0, 0, HALF, product[:], wgo_rows[:, 0:HALF])
        woven_rest = held.tile([P, M - P, PACK], BF16, name="woven_rest", tag="woven_slot", align_bytes=64)
        quantise_up(raw_rest[:, :, 0:P], woven_rest[:, 0:P, :], P)
        quantise_up(raw_rest[:, :, P : 3 * P], woven_rest[:, P : 3 * P, :], 2 * P)
        product = held.tile([P, HALF], F32, name="product1", tag="woven_slot", align_bytes=64)
        gated = held.tile([P, HALF], F32, name="gated0_2")
        first_block_run(HALF, HALF, gated, product[:], gate_bank=0, up_bank=4)
        scatter(0, HALF, HALF, product[:], wgo_rows[:, HALF:S])

        turned = bank("turned", 2, [P, S // P, P])
        for w in range(S // P):
            nc.tensor.transpose(turned[:, w, :], wgo_rows[:, w * P : (w + 1) * P], ident[:])
        for w in range(0, S // P, HALF // P):
            nc.scalar.copy(wgo_cols[:, w : w + HALF // P], turned[:, w : w + HALF // P, 0])

        step = 0
        for b in range(1, BLOCKS):
            width = HALF if b == 1 else S
            for s0 in range(0, S, width):
                gated = held.tile([P, width], F32, name="gated%d_%d" % (b, s0))
                weighted = held.tile([P, width], F32, name="weighted%d_%d" % (b, s0))
                for j0 in range(s0, s0 + width, HALF):
                    cols = slice(j0 - s0, j0 - s0 + HALF)
                    up_t = bank("up_t%d" % step, (step + 2) % 3, [P, HALF // P, P])
                    for c in range(HALF // P):
                        picked = slice(j0 + c * P, j0 + (c + 1) * P)
                        nc.tensor.matmul_mx(out=up_t[:, c, :], lhsT=got_words[:, picked].bitcast(FP8X4), lhsT_scale=got_scales[:, picked],
                                            rhs=up_words[:, b * P : (b + 1) * P].bitcast(FP8X4), rhs_scale=up_scales[:, b * P : (b + 1) * P], start=True, stop=True)
                    weighted_t = held.tile([P, HALF // P, P], F32, name="weighted_t%d" % step, tag="weighted_t%d" % (step % 2))
                    for c in range(HALF // P):
                        w = j0 // P + c
                        nc.scalar.activation(weighted_t[:, c, :], up_t[:, c, :], ACT.Copy, scale=wgo_cols[:, w : w + 1])
                    gated_run(b, j0, HALF, gated[:, cols], 3 + step % 2)
                    back = bank("back%d" % step, 5 + (step + 2) % 3, [P, HALF // P, P])
                    for c in range(HALF // P):
                        nc.tensor.transpose(back[:, c, :], weighted_t[:, c, :], ident[:])
                    nc.scalar.copy(weighted[:, cols], back[:].rearrange("p c n -> p (c n)"))
                    step = step + 1
                scatter(b, s0, width, gated[:], weighted[:])
